import numpy as np
import ml_dtypes


def mxq(x, axis, fmt="e4m3"):
    dtype, down = {"e4m3": (ml_dtypes.float8_e4m3fn, 7), "e5m2": (ml_dtypes.float8_e5m2, 14)}[fmt]
    v = np.moveaxis(np.asarray(x, np.float32).astype(ml_dtypes.bfloat16).astype(np.float64), axis, -1)
    blocks = v.reshape(v.shape[:-1] + (-1, 32))
    amax = np.abs(blocks).max(-1, keepdims=True)
    byte = np.maximum(np.where(amax > 0, np.frexp(amax)[1] - 1 + 127, 0) - down, 1)
    scale = np.exp2(byte - 127.0)
    codes = (blocks / scale).astype(np.float32).astype(dtype).astype(np.float64)
    return np.moveaxis((codes * scale).reshape(v.shape), -1, axis)


WIDE = False


def mx_kscale(k, group=512):
    if not WIDE:
        return np.ones(k)
    levels = np.array([10, -10, 5, -5, 0])
    if group != 512:
        return np.exp2(np.random.permutation(np.resize(levels, k // group))).repeat(group)
    if k % 512:
        return np.exp2(np.random.permutation(np.resize(levels, k // 32))).repeat(32)
    a = np.empty((k // 512, 16))
    for p in range(k // 512):
        a[p, :8] = np.random.permutation(np.resize(levels, 8))
        for g in range(8):
            far = levels[np.abs(levels - a[p, g]) >= 10]
            a[p, g + 8] = far[np.random.randint(len(far))]
    return np.exp2(a.ravel()).repeat(32)


def f64(x):
    return np.asarray(x).astype(np.float64)


E2M1 = np.array([0.0, 0.5, 1.0, 1.5, 2.0, 3.0, 4.0, 6.0, -0.0, -0.5, -1.0, -1.5, -2.0, -3.0, -4.0, -6.0])


def pack_group(w):
    k, n = w.shape
    w = f64(np.asarray(w, np.float32).astype(ml_dtypes.bfloat16)).reshape(k // 32, 32, n)
    amax = np.abs(w).max(1)
    mant, ex = np.frexp(amax / 6.0)
    byte = np.clip(np.where(amax > 0, np.where(mant > 0.5, ex, ex - 1) + 127, 1), 1, 254)
    scaled = (w * np.exp2(127.0 - byte)[:, None, :]).reshape(k, n).astype(np.float32)
    c = np.ascontiguousarray(scaled.reshape(k // 4, 4, n).transpose(0, 2, 1)).astype(ml_dtypes.float4_e2m1fn).view(np.uint8) & 0xF
    return np.ascontiguousarray((c[..., 0::2] | (c[..., 1::2] << 4)).reshape(k // 4, 2 * n)), byte.astype(np.uint8)


def unpack_group(words, scales):
    p, n = words.shape[0], scales.shape[1]
    words = np.ascontiguousarray(words).reshape(p, n, 2)
    nib = np.empty((p, n, 4), np.uint8)
    nib[..., 0::2] = words & 0xF
    nib[..., 1::2] = words >> 4
    return E2M1[nib].transpose(0, 2, 1).reshape(4 * p, n) * np.repeat(np.exp2(scales.astype(np.float64) - 127.0), 32, axis=0)


def sigmoid(v):
    return 1.0 / (1.0 + np.exp(-v))


G, D, M, O, N = 2, 256, 256, 256, 512


def setup_inputs():
    n = np.random.standard_normal
    s_d = mx_kscale(D, 0)
    s_o = mx_kscale(O, 0)
    w1_ = [pack_group(w) for w in n((G, D, M)) / np.sqrt(D) / s_d[:, None]]
    w2_ = [pack_group(w) for w in n((G, D, M)) / np.sqrt(D) / s_d[:, None]]
    w3_ = [pack_group(w) for w in n((G, D, M)) / np.sqrt(D) / s_d[:, None]]
    wo_ = [pack_group(w) for w in n((G, O, M)) / np.sqrt(O) / s_o[:, None]]
    return {
        "x": (n((G, D, N)) * s_d[:, None]).astype(np.float32),
        "w1_words": np.stack([w[0] for w in w1_]),
        "w1_scales": np.stack([w[1] for w in w1_]),
        "w2_words": np.stack([w[0] for w in w2_]),
        "w2_scales": np.stack([w[1] for w in w2_]),
        "w3_words": np.stack([w[0] for w in w3_]),
        "w3_scales": np.stack([w[1] for w in w3_]),
        "th": (0.5 * n((G, M, 1))).astype(np.float32),
        "wo_words": np.stack([w[0] for w in wo_]),
        "wo_scales": np.stack([w[1] for w in wo_]),
        "dy": (n((G, O, N)) * s_o[:, None]).astype(np.float32),
        "old": (0.3 * n((G, M, N))).astype(np.float32),
    }


def reference(x, w1_words, w1_scales, w2_words, w2_scales, w3_words, w3_scales, th, wo_words, wo_scales, dy, old):
    w1 = np.stack([unpack_group(w1_words[g], w1_scales[g]) for g in range(G)])
    xq = mxq(f64(x), 1, "e4m3")
    z1 = w1.transpose(0, 2, 1) @ xq
    w2 = np.stack([unpack_group(w2_words[g], w2_scales[g]) for g in range(G)])
    z2 = w2.transpose(0, 2, 1) @ xq
    w3 = np.stack([unpack_group(w3_words[g], w3_scales[g]) for g in range(G)])
    z3 = w3.transpose(0, 2, 1) @ xq
    g2 = sigmoid(z2)
    g3 = sigmoid(z3 - f64(th))
    wo = np.stack([unpack_group(wo_words[g], wo_scales[g]) for g in range(G)])
    dyq = mxq(f64(dy), 1, "e4m3")
    c0 = wo.transpose(0, 2, 1) @ dyq
    dg2 = c0 * g3 * z1
    dz2 = dg2 * g2 * (1.0 - g2)
    y = dz2 + f64(old)
    return y

@@ -1,0 +1,157 @@
+from contextlib import ExitStack
+
+import concourse.mybir as mybir
+
+G, D, M, N = 2, 256, 256, 512
+FLOPS = 4 * 2 * G * D * M * N
+
+F32 = mybir.dt.float32
+BF16 = mybir.dt.bfloat16
+I32 = mybir.dt.int32
+U32 = mybir.dt.uint32
+U8 = mybir.dt.uint8
+FP8X4 = mybir.dt.float8_e4m3fn_x4
+FP4X4 = mybir.dt.float4_e2m1fn_x4
+ACT = mybir.ActivationFunctionType
+ALU = mybir.AluOpType
+
+P = 128
+PACK = 4
+ROWS = D // PACK
+QUAD = 32
+HALF = N // 2
+X_SCALAR_FROM = 304
+DY_SCALAR_FROM = 336
+
+
+def tile_rows_btwogates_kernel(tc, x, w1_words, w1_scales, w2_words, w2_scales, w3_words, w3_scales, th,
+                                   wo_words, wo_scales, dy, old, out):
+    nc = tc.nc
+    names = ["z3", "z2", "z1", "c0"]
+    words_in = {"z3": w3_words, "z2": w2_words, "z1": w1_words, "c0": wo_words}
+    scales_in = {"z3": w3_scales, "z2": w2_scales, "z1": w1_scales, "c0": wo_scales}
+    tiles = [(g, h) for h in range(M // P) for g in range(G)]
+
+    with ExitStack() as ctx:
+        keep = ctx.enter_context(tc.tile_pool(name="keep", bufs=1))
+        work = ctx.enter_context(tc.tile_pool(name="work", bufs=4))
+        psum = ctx.enter_context(tc.psum_pool(name="psum", bufs=1))
+        ctx.enter_context(tc.manual_schedule())
+
+        planes = keep.tile([P, len(names) * M], U8, align_bytes=64)
+        minus_half = keep.tile([P, 1], F32)
+        warm = keep.tile([P, 1], F32)
+        th_rows = keep.tile([P, P], F32, align_bytes=64)
+        th_cols = keep.tile([P, P], F32, align_bytes=64)
+        minus_th = keep.tile([P, len(tiles)], F32)
+        words = {}
+        for name in names:
+            words[name] = keep.tile([P, 2 * M], U8, align_bytes=64, name="words_" + name)
+        raw, packed, codes, scales = {}, {}, {}, {}
+        for name in ("x", "dy"):
+            raw[name] = keep.tile([P, PACK, N], F32, name="raw_" + name)
+            packed[name] = keep.tile([P, N, PACK], BF16, align_bytes=64, name="packed_" + name)
+            codes[name] = keep.tile([P, N], U32, align_bytes=64, name="codes_" + name)
+            scales[name] = keep.tile([P, N], U8, align_bytes=64, name="scales_" + name)
+        old_sb = []
+        for h in range(M // P):
+            old_sb.append(keep.tile([P, G, N], F32, name="old_%d" % h))
+
+        def load_words(queue, name):
+            queue.dma_start(out=words[name][:].bitcast(I32),
+                            in_=words_in[name].rearrange("g p b -> (g p) b").bitcast(I32))
+
+        def load_rows(name, src):
+            nc.sync.dma_start(out=raw[name][:], in_=src.rearrange("g (p j) n -> (g p) j n", j=PACK))
+
+        def interleave(copy, name, lo, hi):
+            copy(out=packed[name][:, lo:hi, :].rearrange("p (c i) j -> p c j i", i=4),
+                 in_=raw[name][:, :, lo:hi].rearrange("p j (c i) -> p c j i", i=4))
+
+        def quantise(name, lo, hi):
+            nc.vector.quantize_mx(out=codes[name][:, lo:hi].bitcast(FP8X4), scales=scales[name][:, lo:hi],
+                                  in_=packed[name][:, lo:hi, :].rearrange("p n j -> p (n j)"))
+
+        def prepare(name, scalar_from):
+            interleave(nc.vector.tensor_copy, name, 0, HALF)
+            interleave(nc.scalar.copy, name, scalar_from, N)
+            interleave(nc.vector.tensor_copy, name, HALF, scalar_from)
+            quantise(name, 0, HALF)
+            quantise(name, HALF, N)
+
+        sums = {}
+
+        def product(name, t):
+            g, h = tiles[t]
+            rows = slice(ROWS * g, ROWS * (g + 1))
+            moving = "dy" if name == "c0" else "x"
+            col = names.index(name) * M + h * P
+            bank = psum.tile([P, N], F32, name="bank_%s_%d" % (name, g))
+            nc.tensor.matmul_mx(out=bank[:], lhsT=words[name][rows, 2 * P * h:2 * P * (h + 1)].bitcast(FP4X4),
+                                lhsT_scale=planes[rows, col:col + P], rhs=codes[moving][rows, :].bitcast(FP8X4),
+                                rhs_scale=scales[moving][rows, :], start=True, stop=True)
+            sums[name, t] = bank
+
+        g3 = {}
+
+        def second_gate(t):
+            g, h = tiles[t]
+            i = 2 * g + h
+            g3[t] = work.tile([P, N], F32, name="g3")
+            nc.scalar.activation(out=g3[t][:], in_=sums["z3", t][:], func=ACT.Sigmoid, bias=minus_th[:, i:i + 1])
+
+        def finish(t):
+            g, h = tiles[t]
+            g2 = work.tile([P, N], F32, name="g2")
+            sq = work.tile([P, N], F32, name="sq")
+            a = work.tile([P, N], F32, name="a")
+            b = work.tile([P, N], F32, name="b")
+            e = work.tile([P, N], F32, name="e")
+            res = work.tile([P, N], F32, name="res")
+            nc.scalar.activation(out=g2[:], in_=sums["z2", t][:], func=ACT.Sigmoid)
+            nc.scalar.activation(out=sq[:], in_=g2[:], func=ACT.Square, bias=minus_half[:])
+            nc.vector.tensor_tensor(out=a[:], in0=g3[t][:], in1=sums["z1", t][:], op=ALU.mult)
+            nc.vector.scalar_tensor_tensor(out=b[:], in0=sq[:], scalar=-0.25, in1=sums["c0", t][:],
+                                           op0=ALU.add, op1=ALU.mult)
+            nc.vector.tensor_tensor(out=e[:], in0=a[:], in1=b[:], op=ALU.mult)
+            nc.vector.tensor_tensor(out=res[:], in0=old_sb[h][:, g, :], in1=e[:], op=ALU.subtract)
+            nc.sync.dma_start(out=out[g, h * P:(h + 1) * P, :], in_=res[:])
+
+        nc.vector.memset(planes[:].bitcast(I32), 0)
+        nc.vector.memset(minus_half[:], -0.5)
+        nc.gpsimd.memset(th_rows[:], 0.0)
+        nc.gpsimd.dma_start(out=th_rows[0:P:QUAD, :].rearrange("c (i a) -> c i a", a=QUAD),
+                            in_=th.rearrange("g (h c a) o -> c (g h) (a o)", h=M // P, a=QUAD))
+        for w, name in enumerate(names):
+            nc.scalar.dma_start(out=planes[0:16, w * M:(w + 1) * M].bitcast(I32),
+                                in_=scales_in[name].rearrange("g t m -> (g t) m").bitcast(I32))
+        load_rows("x", x)
+        load_words(nc.sync, "z3")
+        load_words(nc.sync, "z2")
+        load_rows("dy", dy)
+        nc.scalar.activation(out=warm[:], in_=minus_half[:], func=ACT.Sigmoid)
+        for q in range(1, P // QUAD):
+            nc.scalar.dma_start(out=planes[QUAD * q:QUAD * q + 4, :].bitcast(I32),
+                                in_=planes[4 * q:4 * q + 4, :].bitcast(I32))
+        load_words(nc.scalar, "z1")
+        load_words(nc.sync, "c0")
+        for h in range(M // P):
+            nc.sync.dma_start(out=old_sb[h][:], in_=old[:, h * P:(h + 1) * P, :].rearrange("g p n -> p g n"))
+
+        prepare("x", X_SCALAR_FROM)
+        nc.vector.transpose(out=th_cols[:], in_=th_rows[:])
+        nc.vector.tensor_scalar(out=minus_th[:], in0=th_cols[:, 0:P:QUAD], scalar1=-1.0, scalar2=None, op0=ALU.mult)
+        for name in names[:3]:
+            for t in range(G):
+                product(name, t)
+        second_gate(0)
+        prepare("dy", DY_SCALAR_FROM)
+        for t in range(G):
+            product("c0", t)
+        for t in range(len(tiles)):
+            finish(t)
+            if t + G < len(tiles):
+                for name in names:
+                    product(name, t + G)
+            if t + 1 < len(tiles):
+                second_gate(t + 1)

@@ -21,7 +21,7 @@ ROWS = D // PACK
 QUAD = 32
 HALF = N // 2
 X_SCALAR_FROM = 304
-DY_SCALAR_FROM = 336
+DY_SCALAR_FROM = 400
 
 
 def tile_rows_btwogates_kernel(tc, x, w1_words, w1_scales, w2_words, w2_scales, w3_words, w3_scales, th,
@@ -39,6 +39,7 @@ def tile_rows_btwogates_kernel(tc, x, w1_words, w1_scales, w2_words, w2_scales, 
         ctx.enter_context(tc.manual_schedule())
 
         planes = keep.tile([P, len(names) * M], U8, align_bytes=64)
+        rows16 = keep.tile([16, len(names) * M], U8)
         minus_half = keep.tile([P, 1], F32)
         warm = keep.tile([P, 1], F32)
         th_rows = keep.tile([P, P], F32, align_bytes=64)
@@ -61,8 +62,8 @@ def tile_rows_btwogates_kernel(tc, x, w1_words, w1_scales, w2_words, w2_scales, 
             queue.dma_start(out=words[name][:].bitcast(I32),
                             in_=words_in[name].rearrange("g p b -> (g p) b").bitcast(I32))
 
-        def load_rows(name, src):
-            nc.sync.dma_start(out=raw[name][:], in_=src.rearrange("g (p j) n -> (g p) j n", j=PACK))
+        def load_rows(queue, name, src):
+            queue.dma_start(out=raw[name][:], in_=src.rearrange("g (p j) n -> (g p) j n", j=PACK))
 
         def interleave(copy, name, lo, hi):
             copy(out=packed[name][:, lo:hi, :].rearrange("p (c i) j -> p c j i", i=4),
@@ -92,66 +93,98 @@ def tile_rows_btwogates_kernel(tc, x, w1_words, w1_scales, w2_words, w2_scales, 
                                 rhs_scale=scales[moving][rows, :], start=True, stop=True)
             sums[name, t] = bank
 
-        g3 = {}
+        g2, g3, sq, a, b, e = {}, {}, {}, {}, {}, {}
 
-        def second_gate(t):
+        def first_gate(t):
+            g2[t] = work.tile([P, N], F32, name="g2")
+            nc.scalar.activation(out=g2[t][:], in_=sums["z2", t][:], func=ACT.Sigmoid)
+
+        def gates(t):
             g, h = tiles[t]
             i = 2 * g + h
             g3[t] = work.tile([P, N], F32, name="g3")
+            sq[t] = work.tile([P, N], F32, name="sq")
             nc.scalar.activation(out=g3[t][:], in_=sums["z3", t][:], func=ACT.Sigmoid, bias=minus_th[:, i:i + 1])
+            nc.scalar.activation(out=sq[t][:], in_=g2[t][:], func=ACT.Square, bias=minus_half[:])
 
-        def finish(t):
-            g, h = tiles[t]
-            g2 = work.tile([P, N], F32, name="g2")
-            sq = work.tile([P, N], F32, name="sq")
-            a = work.tile([P, N], F32, name="a")
-            b = work.tile([P, N], F32, name="b")
-            e = work.tile([P, N], F32, name="e")
-            res = work.tile([P, N], F32, name="res")
-            nc.scalar.activation(out=g2[:], in_=sums["z2", t][:], func=ACT.Sigmoid)
-            nc.scalar.activation(out=sq[:], in_=g2[:], func=ACT.Square, bias=minus_half[:])
-            nc.vector.tensor_tensor(out=a[:], in0=g3[t][:], in1=sums["z1", t][:], op=ALU.mult)
-            nc.vector.scalar_tensor_tensor(out=b[:], in0=sq[:], scalar=-0.25, in1=sums["c0", t][:],
+        def value(t):
+            a[t] = work.tile([P, N], F32, name="a")
+            nc.vector.tensor_tensor(out=a[t][:], in0=g3[t][:], in1=sums["z1", t][:], op=ALU.mult)
+
+        def slope(t):
+            b[t] = work.tile([P, N], F32, name="b")
+            nc.vector.scalar_tensor_tensor(out=b[t][:], in0=sq[t][:], scalar=-0.25, in1=sums["c0", t][:],
                                            op0=ALU.add, op1=ALU.mult)
-            nc.vector.tensor_tensor(out=e[:], in0=a[:], in1=b[:], op=ALU.mult)
-            nc.vector.tensor_tensor(out=res[:], in0=old_sb[h][:, g, :], in1=e[:], op=ALU.subtract)
-            nc.sync.dma_start(out=out[g, h * P:(h + 1) * P, :], in_=res[:])
 
-        nc.vector.memset(planes[:].bitcast(I32), 0)
+        def join(t, parts):
+            e[t] = work.tile([P, N], F32, name="e")
+            for cols in parts:
+                nc.vector.tensor_tensor(out=e[t][:, cols], in0=a[t][:, cols], in1=b[t][:, cols], op=ALU.mult)
+
+        def finish(t, parts):
+            g, h = tiles[t]
+            res = work.tile([P, N], F32, name="res")
+            for cols in parts:
+                nc.vector.tensor_tensor(out=res[:, cols], in0=old_sb[h][:, g, cols], in1=e[t][:, cols], op=ALU.subtract)
+                nc.sync.dma_start(out=out[g, h * P:(h + 1) * P, cols], in_=res[:, cols])
+
+        def load_scales(queue, name):
+            w = names.index(name)
+            queue.dma_start(out=rows16[:, w * M:(w + 1) * M].bitcast(I32),
+                            in_=scales_in[name].rearrange("g t m -> (g t) m").bitcast(I32))
+
         nc.vector.memset(minus_half[:], -0.5)
+        nc.vector.memset(planes[:].bitcast(I32), 0)
         nc.gpsimd.memset(th_rows[:], 0.0)
         nc.gpsimd.dma_start(out=th_rows[0:P:QUAD, :].rearrange("c (i a) -> c i a", a=QUAD),
                             in_=th.rearrange("g (h c a) o -> c (g h) (a o)", h=M // P, a=QUAD))
-        for w, name in enumerate(names):
-            nc.scalar.dma_start(out=planes[0:16, w * M:(w + 1) * M].bitcast(I32),
-                                in_=scales_in[name].rearrange("g t m -> (g t) m").bitcast(I32))
-        load_rows("x", x)
-        load_words(nc.sync, "z3")
-        load_words(nc.sync, "z2")
-        load_rows("dy", dy)
+        load_scales(nc.sync, "z2")
+        load_scales(nc.scalar, "z1")
+        load_scales(nc.sync, "z3")
+        load_scales(nc.scalar, "c0")
+        load_rows(nc.sync, "x", x)
+        for name in ("z2", "z3"):
+            load_words(nc.sync, name)
         nc.scalar.activation(out=warm[:], in_=minus_half[:], func=ACT.Sigmoid)
-        for q in range(1, P // QUAD):
+        for q in range(P // QUAD):
             nc.scalar.dma_start(out=planes[QUAD * q:QUAD * q + 4, :].bitcast(I32),
-                                in_=planes[4 * q:4 * q + 4, :].bitcast(I32))
-        load_words(nc.scalar, "z1")
-        load_words(nc.sync, "c0")
-        for h in range(M // P):
-            nc.sync.dma_start(out=old_sb[h][:], in_=old[:, h * P:(h + 1) * P, :].rearrange("g p n -> p g n"))
+                                in_=rows16[4 * q:4 * q + 4, :].bitcast(I32))
+        load_rows(nc.scalar, "dy", dy)
 
         prepare("x", X_SCALAR_FROM)
+        load_words(nc.scalar, "z1")
+        load_words(nc.scalar, "c0")
+        for h in range(M // P):
+            nc.scalar.dma_start(out=old_sb[h][:], in_=old[:, h * P:(h + 1) * P, :].rearrange("g p n -> p g n"))
         nc.vector.transpose(out=th_cols[:], in_=th_rows[:])
         nc.vector.tensor_scalar(out=minus_th[:], in0=th_cols[:, 0:P:QUAD], scalar1=-1.0, scalar2=None, op0=ALU.mult)
-        for name in names[:3]:
-            for t in range(G):
-                product(name, t)
-        second_gate(0)
-        prepare("dy", DY_SCALAR_FROM)
-        for t in range(G):
+        last = len(tiles) - 1
+        whole = [slice(0, N)]
+        halves = [slice(0, HALF), slice(HALF, N)]
+
+        def products(t):
+            if t < last:
+                product("z2", t + 1)
+            product("z1", t)
+            if t < last:
+                product("z3", t + 1)
             product("c0", t)
-        for t in range(len(tiles)):
-            finish(t)
-            if t + G < len(tiles):
-                for name in names:
-                    product(name, t + G)
-            if t + 1 < len(tiles):
-                second_gate(t + 1)
+
+        product("z2", 0)
+        product("z3", 0)
+        first_gate(0)
+        prepare("dy", DY_SCALAR_FROM)
+        products(0)
+        gates(0)
+        value(0)
+        slope(0)
+        for t in range(last):
+            products(t + 1)
+            first_gate(t + 1)
+            gates(t + 1)
+            value(t + 1)
+            join(t, whole)
+            slope(t + 1)
+            finish(t, whole)
+        join(last, halves)
+        finish(last, halves)

@@ -22,6 +22,7 @@ QUAD = 32
 HALF = N // 2
 X_SCALAR_FROM = 304
 DY_SCALAR_FROM = 400
+GPSIMD_COLS = 384
 
 
 def tile_rows_btwogates_kernel(tc, x, w1_words, w1_scales, w2_words, w2_scales, w3_words, w3_scales, th,
@@ -93,18 +94,20 @@ def tile_rows_btwogates_kernel(tc, x, w1_words, w1_scales, w2_words, w2_scales, 
                                 rhs_scale=scales[moving][rows, :], start=True, stop=True)
             sums[name, t] = bank
 
-        g2, g3, sq, a, b, e = {}, {}, {}, {}, {}, {}
+        g2, g3, sq, a, b, e, res = {}, {}, {}, {}, {}, {}, {}
+
+        def second_gate(t):
+            g, h = tiles[t]
+            i = 2 * g + h
+            g3[t] = work.tile([P, N], F32, name="g3")
+            nc.scalar.activation(out=g3[t][:], in_=sums["z3", t][:], func=ACT.Sigmoid, bias=minus_th[:, i:i + 1])
 
         def first_gate(t):
             g2[t] = work.tile([P, N], F32, name="g2")
             nc.scalar.activation(out=g2[t][:], in_=sums["z2", t][:], func=ACT.Sigmoid)
 
-        def gates(t):
-            g, h = tiles[t]
-            i = 2 * g + h
-            g3[t] = work.tile([P, N], F32, name="g3")
+        def square(t):
             sq[t] = work.tile([P, N], F32, name="sq")
-            nc.scalar.activation(out=g3[t][:], in_=sums["z3", t][:], func=ACT.Sigmoid, bias=minus_th[:, i:i + 1])
             nc.scalar.activation(out=sq[t][:], in_=g2[t][:], func=ACT.Square, bias=minus_half[:])
 
         def value(t):
@@ -118,73 +121,84 @@ def tile_rows_btwogates_kernel(tc, x, w1_words, w1_scales, w2_words, w2_scales, 
 
         def join(t, parts):
             e[t] = work.tile([P, N], F32, name="e")
+            res[t] = work.tile([P, N], F32, name="res")
             for cols in parts:
                 nc.vector.tensor_tensor(out=e[t][:, cols], in0=a[t][:, cols], in1=b[t][:, cols], op=ALU.mult)
 
-        def finish(t, parts):
+        def subtract(engine, t, cols):
             g, h = tiles[t]
-            res = work.tile([P, N], F32, name="res")
-            for cols in parts:
-                nc.vector.tensor_tensor(out=res[:, cols], in0=old_sb[h][:, g, cols], in1=e[t][:, cols], op=ALU.subtract)
-                nc.sync.dma_start(out=out[g, h * P:(h + 1) * P, cols], in_=res[:, cols])
+            engine.tensor_tensor(out=res[t][:, cols], in0=old_sb[h][:, g, cols], in1=e[t][:, cols], op=ALU.subtract)
+
+        def store(t, cols):
+            g, h = tiles[t]
+            nc.sync.dma_start(out=out[g, h * P:(h + 1) * P, cols], in_=res[t][:, cols])
 
         def load_scales(queue, name):
             w = names.index(name)
             queue.dma_start(out=rows16[:, w * M:(w + 1) * M].bitcast(I32),
                             in_=scales_in[name].rearrange("g t m -> (g t) m").bitcast(I32))
 
+        def spread_scales(queue, q):
+            queue.dma_start(out=planes[QUAD * q:QUAD * q + 4, :].bitcast(I32),
+                            in_=rows16[4 * q:4 * q + 4, :].bitcast(I32))
+
         nc.vector.memset(minus_half[:], -0.5)
         nc.vector.memset(planes[:].bitcast(I32), 0)
         nc.gpsimd.memset(th_rows[:], 0.0)
         nc.gpsimd.dma_start(out=th_rows[0:P:QUAD, :].rearrange("c (i a) -> c i a", a=QUAD),
                             in_=th.rearrange("g (h c a) o -> c (g h) (a o)", h=M // P, a=QUAD))
-        load_scales(nc.sync, "z2")
-        load_scales(nc.scalar, "z1")
         load_scales(nc.sync, "z3")
+        load_scales(nc.scalar, "z1")
+        load_scales(nc.sync, "z2")
         load_scales(nc.scalar, "c0")
         load_rows(nc.sync, "x", x)
-        for name in ("z2", "z3"):
+        for name in ("z3", "z2"):
             load_words(nc.sync, name)
         nc.scalar.activation(out=warm[:], in_=minus_half[:], func=ACT.Sigmoid)
         for q in range(P // QUAD):
-            nc.scalar.dma_start(out=planes[QUAD * q:QUAD * q + 4, :].bitcast(I32),
-                                in_=rows16[4 * q:4 * q + 4, :].bitcast(I32))
-        load_rows(nc.scalar, "dy", dy)
+            spread_scales(nc.scalar if q % 2 else nc.sync, q)
+        load_rows(nc.sync, "dy", dy)
+        for name in ("z1", "c0"):
+            load_words(nc.sync, name)
+        for h in range(M // P):
+            nc.sync.dma_start(out=old_sb[h][:], in_=old[:, h * P:(h + 1) * P, :].rearrange("g p n -> p g n"))
 
         prepare("x", X_SCALAR_FROM)
-        load_words(nc.scalar, "z1")
-        load_words(nc.scalar, "c0")
-        for h in range(M // P):
-            nc.scalar.dma_start(out=old_sb[h][:], in_=old[:, h * P:(h + 1) * P, :].rearrange("g p n -> p g n"))
         nc.vector.transpose(out=th_cols[:], in_=th_rows[:])
         nc.vector.tensor_scalar(out=minus_th[:], in0=th_cols[:, 0:P:QUAD], scalar1=-1.0, scalar2=None, op0=ALU.mult)
         last = len(tiles) - 1
-        whole = [slice(0, N)]
-        halves = [slice(0, HALF), slice(HALF, N)]
+        whole = slice(0, N)
+        tail = [slice(0, N - P), slice(N - P, N)]
 
-        def products(t):
-            if t < last:
-                product("z2", t + 1)
-            product("z1", t)
-            if t < last:
-                product("z3", t + 1)
-            product("c0", t)
-
-        product("z2", 0)
         product("z3", 0)
-        first_gate(0)
+        product("z2", 0)
+        product("z1", 0)
+        product("z2", 1)
+        product("z3", 1)
+        second_gate(0)
         prepare("dy", DY_SCALAR_FROM)
-        products(0)
-        gates(0)
+        product("c0", 0)
+        first_gate(0)
+        square(0)
         value(0)
         slope(0)
-        for t in range(last):
-            products(t + 1)
-            first_gate(t + 1)
-            gates(t + 1)
-            value(t + 1)
-            join(t, whole)
-            slope(t + 1)
-            finish(t, whole)
-        join(last, halves)
-        finish(last, halves)
+        for t in range(1, last + 1):
+            join(t - 1, [whole])
+            subtract(nc.gpsimd, t - 1, slice(0, GPSIMD_COLS))
+            first_gate(t)
+            second_gate(t)
+            square(t)
+            product("z1", t)
+            if t < last:
+                product("z2", t + 1)
+            product("c0", t)
+            if t < last:
+                product("z3", t + 1)
+            value(t)
+            slope(t)
+            subtract(nc.vector, t - 1, slice(GPSIMD_COLS, N))
+            store(t - 1, whole)
+        join(last, tail)
+        for cols in tail:
+            subtract(nc.vector, last, cols)
+            store(last, cols)

from contextlib import ExitStack

import concourse.mybir as mybir

G, D, M, N = 2, 256, 256, 512
FLOPS = 4 * 2 * G * D * M * N

F32 = mybir.dt.float32
BF16 = mybir.dt.bfloat16
I32 = mybir.dt.int32
U32 = mybir.dt.uint32
U8 = mybir.dt.uint8
FP8X4 = mybir.dt.float8_e4m3fn_x4
FP4X4 = mybir.dt.float4_e2m1fn_x4
ACT = mybir.ActivationFunctionType
ALU = mybir.AluOpType

P = 128
PACK = 4
ROWS = D // PACK
QUAD = 32
HALF = N // 2
X_SCALAR_FROM = 304
DY_SCALAR_FROM = 400
GPSIMD_COLS = 384


def tile_rows_btwogates_kernel(tc, x, w1_words, w1_scales, w2_words, w2_scales, w3_words, w3_scales, th,
                                   wo_words, wo_scales, dy, old, out):
    nc = tc.nc
    names = ["z3", "z2", "z1", "c0"]
    words_in = {"z3": w3_words, "z2": w2_words, "z1": w1_words, "c0": wo_words}
    scales_in = {"z3": w3_scales, "z2": w2_scales, "z1": w1_scales, "c0": wo_scales}
    tiles = [(g, h) for h in range(M // P) for g in range(G)]

    with ExitStack() as ctx:
        keep = ctx.enter_context(tc.tile_pool(name="keep", bufs=1))
        work = ctx.enter_context(tc.tile_pool(name="work", bufs=4))
        psum = ctx.enter_context(tc.psum_pool(name="psum", bufs=1))
        ctx.enter_context(tc.manual_schedule())

        planes = keep.tile([P, len(names) * M], U8, align_bytes=64)
        rows16 = keep.tile([16, len(names) * M], U8)
        minus_half = keep.tile([P, 1], F32)
        warm = keep.tile([P, 1], F32)
        th_rows = keep.tile([P, P], F32, align_bytes=64)
        th_cols = keep.tile([P, P], F32, align_bytes=64)
        minus_th = keep.tile([P, len(tiles)], F32)
        words = {}
        for name in names:
            words[name] = keep.tile([P, 2 * M], U8, align_bytes=64, name="words_" + name)
        raw, packed, codes, scales = {}, {}, {}, {}
        for name in ("x", "dy"):
            raw[name] = keep.tile([P, PACK, N], F32, name="raw_" + name)
            packed[name] = keep.tile([P, N, PACK], BF16, align_bytes=64, name="packed_" + name)
            codes[name] = keep.tile([P, N], U32, align_bytes=64, name="codes_" + name)
            scales[name] = keep.tile([P, N], U8, align_bytes=64, name="scales_" + name)
        old_sb = []
        for h in range(M // P):
            old_sb.append(keep.tile([P, G, N], F32, name="old_%d" % h))

        def load_words(queue, name):
            queue.dma_start(out=words[name][:].bitcast(I32),
                            in_=words_in[name].rearrange("g p b -> (g p) b").bitcast(I32))

        def load_rows(queue, name, src):
            queue.dma_start(out=raw[name][:], in_=src.rearrange("g (p j) n -> (g p) j n", j=PACK))

        def interleave(copy, name, lo, hi):
            copy(out=packed[name][:, lo:hi, :].rearrange("p (c i) j -> p c j i", i=4),
                 in_=raw[name][:, :, lo:hi].rearrange("p j (c i) -> p c j i", i=4))

        def quantise(name, lo, hi):
            nc.vector.quantize_mx(out=codes[name][:, lo:hi].bitcast(FP8X4), scales=scales[name][:, lo:hi],
                                  in_=packed[name][:, lo:hi, :].rearrange("p n j -> p (n j)"))

        def prepare(name, scalar_from):
            interleave(nc.vector.tensor_copy, name, 0, HALF)
            interleave(nc.scalar.copy, name, scalar_from, N)
            interleave(nc.vector.tensor_copy, name, HALF, scalar_from)
            quantise(name, 0, HALF)
            quantise(name, HALF, N)

        sums = {}

        def product(name, t):
            g, h = tiles[t]
            rows = slice(ROWS * g, ROWS * (g + 1))
            moving = "dy" if name == "c0" else "x"
            col = names.index(name) * M + h * P
            bank = psum.tile([P, N], F32, name="bank_%s_%d" % (name, g))
            nc.tensor.matmul_mx(out=bank[:], lhsT=words[name][rows, 2 * P * h:2 * P * (h + 1)].bitcast(FP4X4),
                                lhsT_scale=planes[rows, col:col + P], rhs=codes[moving][rows, :].bitcast(FP8X4),
                                rhs_scale=scales[moving][rows, :], start=True, stop=True)
            sums[name, t] = bank

        g2, g3, sq, a, b, e, res = {}, {}, {}, {}, {}, {}, {}

        def second_gate(t):
            g, h = tiles[t]
            i = 2 * g + h
            g3[t] = work.tile([P, N], F32, name="g3")
            nc.scalar.activation(out=g3[t][:], in_=sums["z3", t][:], func=ACT.Sigmoid, bias=minus_th[:, i:i + 1])

        def first_gate(t):
            g2[t] = work.tile([P, N], F32, name="g2")
            nc.scalar.activation(out=g2[t][:], in_=sums["z2", t][:], func=ACT.Sigmoid)

        def square(t):
            sq[t] = work.tile([P, N], F32, name="sq")
            nc.scalar.activation(out=sq[t][:], in_=g2[t][:], func=ACT.Square, bias=minus_half[:])

        def value(t):
            a[t] = work.tile([P, N], F32, name="a")
            nc.vector.tensor_tensor(out=a[t][:], in0=g3[t][:], in1=sums["z1", t][:], op=ALU.mult)

        def slope(t):
            b[t] = work.tile([P, N], F32, name="b")
            nc.vector.scalar_tensor_tensor(out=b[t][:], in0=sq[t][:], scalar=-0.25, in1=sums["c0", t][:],
                                           op0=ALU.add, op1=ALU.mult)

        def join(t, parts):
            e[t] = work.tile([P, N], F32, name="e")
            res[t] = work.tile([P, N], F32, name="res")
            for cols in parts:
                nc.vector.tensor_tensor(out=e[t][:, cols], in0=a[t][:, cols], in1=b[t][:, cols], op=ALU.mult)

        def subtract(engine, t, cols):
            g, h = tiles[t]
            engine.tensor_tensor(out=res[t][:, cols], in0=old_sb[h][:, g, cols], in1=e[t][:, cols], op=ALU.subtract)

        def store(t, cols):
            g, h = tiles[t]
            nc.sync.dma_start(out=out[g, h * P:(h + 1) * P, cols], in_=res[t][:, cols])

        def load_scales(queue, name):
            w = names.index(name)
            queue.dma_start(out=rows16[:, w * M:(w + 1) * M].bitcast(I32),
                            in_=scales_in[name].rearrange("g t m -> (g t) m").bitcast(I32))

        def spread_scales(queue, q):
            queue.dma_start(out=planes[QUAD * q:QUAD * q + 4, :].bitcast(I32),
                            in_=rows16[4 * q:4 * q + 4, :].bitcast(I32))

        nc.vector.memset(minus_half[:], -0.5)
        nc.vector.memset(planes[:].bitcast(I32), 0)
        nc.gpsimd.memset(th_rows[:], 0.0)
        nc.gpsimd.dma_start(out=th_rows[0:P:QUAD, :].rearrange("c (i a) -> c i a", a=QUAD),
                            in_=th.rearrange("g (h c a) o -> c (g h) (a o)", h=M // P, a=QUAD))
        load_scales(nc.sync, "z3")
        load_scales(nc.scalar, "z1")
        load_scales(nc.sync, "z2")
        load_scales(nc.scalar, "c0")
        load_rows(nc.sync, "x", x)
        for name in ("z3", "z2"):
            load_words(nc.sync, name)
        nc.scalar.activation(out=warm[:], in_=minus_half[:], func=ACT.Sigmoid)
        for q in range(P // QUAD):
            spread_scales(nc.scalar if q % 2 else nc.sync, q)
        load_rows(nc.sync, "dy", dy)
        for name in ("z1", "c0"):
            load_words(nc.sync, name)
        for h in range(M // P):
            nc.sync.dma_start(out=old_sb[h][:], in_=old[:, h * P:(h + 1) * P, :].rearrange("g p n -> p g n"))

        prepare("x", X_SCALAR_FROM)
        nc.vector.transpose(out=th_cols[:], in_=th_rows[:])
        nc.vector.tensor_scalar(out=minus_th[:], in0=th_cols[:, 0:P:QUAD], scalar1=-1.0, scalar2=None, op0=ALU.mult)
        last = len(tiles) - 1
        whole = slice(0, N)
        tail = [slice(0, N - P), slice(N - P, N)]

        product("z3", 0)
        product("z2", 0)
        product("z1", 0)
        product("z2", 1)
        product("z3", 1)
        second_gate(0)
        prepare("dy", DY_SCALAR_FROM)
        product("c0", 0)
        first_gate(0)
        square(0)
        value(0)
        slope(0)
        for t in range(1, last + 1):
            join(t - 1, [whole])
            subtract(nc.gpsimd, t - 1, slice(0, GPSIMD_COLS))
            first_gate(t)
            second_gate(t)
            square(t)
            product("z1", t)
            if t < last:
                product("z2", t + 1)
            product("c0", t)
            if t < last:
                product("z3", t + 1)
            value(t)
            slope(t)
            subtract(nc.vector, t - 1, slice(GPSIMD_COLS, N))
            store(t - 1, whole)
        join(last, tail)
        for cols in tail:
            subtract(nc.vector, last, cols)
            store(last, cols)
